import numpy as np
import ml_dtypes


def mxq(x, axis, fmt="e4m3"):
    dtype, down = {"e4m3": (ml_dtypes.float8_e4m3fn, 7), "e5m2": (ml_dtypes.float8_e5m2, 14)}[fmt]
    v = np.moveaxis(np.asarray(x, np.float32).astype(ml_dtypes.bfloat16).astype(np.float64), axis, -1)
    blocks = v.reshape(v.shape[:-1] + (-1, 32))
    amax = np.abs(blocks).max(-1, keepdims=True)
    byte = np.maximum(np.where(amax > 0, np.frexp(amax)[1] - 1 + 127, 0) - down, 1)
    scale = np.exp2(byte - 127.0)
    codes = (blocks / scale).astype(np.float32).astype(dtype).astype(np.float64)
    return np.moveaxis((codes * scale).reshape(v.shape), -1, axis)


WIDE = False


def mx_kscale(k):
    if not WIDE:
        return np.ones(k)
    levels = np.array([10, -10, 5, -5, 0])
    if k % 512:
        return np.exp2(np.random.permutation(np.resize(levels, k // 32))).repeat(32)
    a = np.empty((k // 512, 16))
    for p in range(k // 512):
        a[p, :8] = np.random.permutation(np.resize(levels, 8))
        for g in range(8):
            far = levels[np.abs(levels - a[p, g]) >= 10]
            a[p, g + 8] = far[np.random.randint(len(far))]
    return np.exp2(a.ravel()).repeat(32)


def f64(x):
    return np.asarray(x).astype(np.float64)


def striped(idx):
    return np.tile(idx.reshape(-1, 16).T, (8, 1)).astype(np.uint16)


def unstriped(offs):
    return offs[:16].T.reshape(-1).astype(np.int64)


def striped8(idx):
    return np.concatenate([x.reshape(-1, 16).T for x in idx]).astype(np.uint16)


def runs(offs, k):
    lists = np.stack([offs[16 * r : 16 * r + 16].T.reshape(-1) for r in range(8)]).astype(np.int64)
    return lists[np.arange(k) % 512 // 64]


def pack_weight(w):
    k, n = w.shape
    w = f64(np.asarray(w, np.float32).astype(ml_dtypes.bfloat16)).reshape(k // 32, 32, n)
    amax = np.abs(w).max(1)
    byte = np.clip(np.where(amax > 0, np.frexp(amax)[1] - 1 + 127 - 7, 1), 1, 254)
    scaled = (w * np.exp2(127.0 - byte)[:, None, :]).reshape(k, n).astype(np.float32)
    words = np.ascontiguousarray(scaled.reshape(k // 512, 128, 4, n).transpose(0, 1, 3, 2)).astype(ml_dtypes.float8_e4m3fn).view(np.uint8)
    return words, np.ascontiguousarray(byte.astype(np.uint8).reshape(k // 512, 16, n))


def unpack_weight(words, scales):
    g, p, n, _ = words.shape
    vals = np.ascontiguousarray(words).view(ml_dtypes.float8_e4m3fn).astype(np.float64) * np.repeat(np.exp2(scales.astype(np.float64) - 127.0), 8, axis=1)[..., None]
    return vals.transpose(0, 1, 3, 2).reshape(g * 512, n)


E2M1 = np.array([0.0, 0.5, 1.0, 1.5, 2.0, 3.0, 4.0, 6.0, -0.0, -0.5, -1.0, -1.5, -2.0, -3.0, -4.0, -6.0])


def pack_fp4(w):
    k, n = w.shape
    w = f64(np.asarray(w, np.float32).astype(ml_dtypes.bfloat16)).reshape(k // 32, 32, n)
    amax = np.abs(w).max(1)
    mant, ex = np.frexp(amax / 6.0)
    byte = np.clip(np.where(amax > 0, np.where(mant > 0.5, ex, ex - 1) + 127, 1), 1, 254)
    scaled = (w * np.exp2(127.0 - byte)[:, None, :]).reshape(k, n).astype(np.float32)
    c = np.ascontiguousarray(scaled.reshape(k // 512, 128, 4, n).transpose(0, 1, 3, 2)).astype(ml_dtypes.float4_e2m1fn).view(np.uint8) & 0xF
    words = (c[..., 0::2] | (c[..., 1::2] << 4)).reshape(k // 512, 128, 2 * n)
    return np.ascontiguousarray(words), np.ascontiguousarray(byte.astype(np.uint8).reshape(k // 512, 16, n))


def unpack_fp4(words, scales):
    g, _, n = scales.shape
    words = np.ascontiguousarray(words).reshape(g, 128, n, 2)
    nib = np.empty((g, 128, n, 4), np.uint8)
    nib[..., 0::2] = words & 0xF
    nib[..., 1::2] = words >> 4
    vals = E2M1[nib] * np.repeat(np.exp2(scales.astype(np.float64) - 127.0), 8, axis=1)[..., None]
    return vals.transpose(0, 1, 3, 2).reshape(g * 512, n)


def planes(y):
    n, m = y.shape
    v = y.astype(np.float32).astype(ml_dtypes.bfloat16).astype(np.float64).reshape(n // 32, 32, m)
    top = np.abs(v).max(1)
    byte = np.clip(np.where(top > 0, np.frexp(top)[1] - 1 + 127 - 7, 1), 1, 254)
    codes = (v * np.exp2(127.0 - byte)[:, None, :]).reshape(n, m).astype(np.float32).astype(ml_dtypes.float8_e4m3fn).view(np.uint8)
    words = codes.reshape(n // 512, 128, 4, m).transpose(0, 1, 3, 2)
    return np.ascontiguousarray(words), np.ascontiguousarray(byte.astype(np.uint8).reshape(n // 512, 16, m))


K, T, S, N, H, G, W = 512, 2048, 512, 512, 512, 2048, 256


def setup_inputs():
    n = np.random.standard_normal
    s = mx_kscale(K)[:, None]
    u = mx_kscale(S)
    packed_xT = pack_weight(n((K, T)) * s)
    packed_w1 = pack_fp4(n((K, H)) / np.sqrt(K) / s)
    packed_dT = pack_weight(n((K, G)) / s)
    packed_w2 = pack_fp4(n((H, N)) / np.sqrt(H) / u[:, None])
    perm = np.stack([np.random.permutation(S) for _ in range(8)])
    return {
        "x_words": packed_xT[0],
        "x_scales": packed_xT[1],
        "w1_words": packed_w1[0],
        "w1_scales": packed_w1[1],
        "d_words": packed_dT[0],
        "d_scales": packed_dT[1],
        "gn": (np.random.uniform(0.5, 1.5, (H, 1)) * u[:, None]).astype(np.float32),
        "w2_words": packed_w2[0],
        "w2_scales": packed_w2[1],
        "offs": striped(np.random.permutation(T)[:S]),
        "k1": striped8(np.random.randint(0, G, (8, H))),
        "two": striped(np.random.permutation(T)[:S]),
        "n1": striped8(np.stack([np.random.permutation(S)[:W] for _ in range(8)])),
        "n2": striped8(np.stack([np.random.permutation(S)[:W] for _ in range(8)])),
        "n3": striped8(perm[:, :W]),
        "n4": striped8(perm[:, W:]),
    }


def reference(x_words, x_scales, w1_words, w1_scales, d_words, d_scales, gn, w2_words, w2_scales, offs, k1, two, n1, n2, n3, n4):
    d_k1 = unpack_weight(d_words, d_scales)[np.arange(K)[:, None], runs(k1, K)]
    x_two = unpack_weight(x_words, x_scales)[:, unstriped(two)]
    d = 0.0625 * (d_k1.T @ x_two)
    xq = unpack_weight(x_words, x_scales)[:, unstriped(offs)]
    y = unpack_fp4(w1_words, w1_scales).T @ xq
    ra = d[np.arange(H)[:, None], runs(n2, H)] - (0.5 * (y[np.arange(H)[:, None], runs(n1, H)]))
    ds = y.copy()
    ds[np.arange(H)[:, None], runs(n1, H)] = ra
    z = f64(gn) * ds
    h = unpack_fp4(w2_words, w2_scales).T @ mxq(z, 0, "e4m3")
    pa = h[np.arange(N)[:, None], runs(n3, N)]
    pb = h[np.arange(N)[:, None], runs(n4, N)]
    ra2 = np.maximum(pa, pb)
    out = h.copy()
    out[np.arange(N)[:, None], runs(n3, N)] = ra2
    return (out,) + planes(out)

@@ -1,0 +1,225 @@
+from contextlib import ExitStack
+
+import concourse.mybir as mybir
+
+F32 = mybir.dt.float32
+BF16 = mybir.dt.bfloat16
+I32 = mybir.dt.int32
+U32 = mybir.dt.uint32
+U16 = mybir.dt.uint16
+U8 = mybir.dt.uint8
+FP8X4 = mybir.dt.float8_e4m3fn_x4
+FP4X4 = mybir.dt.float4_e2m1fn_x4
+COPY = mybir.ActivationFunctionType.Copy
+ADD = mybir.AluOpType.add
+MULT = mybir.AluOpType.mult
+MAX = mybir.AluOpType.max
+
+P = 128
+PACK = 4
+TABLE = 2048
+S = 512
+HALF = S // 2
+W = 256
+FLOPS = 3 * 2 * 512 * 512 * 512
+
+
+def tile_picked_twkeyputbfill_none_po_kernel(
+    tc, x_words, x_scales, w1_words, w1_scales, d_words, d_scales, gn, w2_words, w2_scales,
+    offs, k1, two, n1, n2, n3, n4, out_0, out_1, out_2,
+):
+    nc = tc.nc
+    halves = [slice(0, HALF), slice(HALF, S)]
+
+    with ExitStack() as ctx:
+        keep = ctx.enter_context(tc.tile_pool(name="keep", bufs=1))
+        psum = ctx.enter_context(tc.psum_pool(name="psum", bufs=8))
+
+        def tile(name, shape, dtype):
+            return keep.tile(shape, dtype, name=name, align_bytes=64)
+
+        def bank(width):
+            return psum.tile([P, width], F32, name="bank")
+
+        def load_list(name, src):
+            dst = tile(name, list(src.shape), U16)
+            nc.sync.dma_start(dst[:], src)
+            return dst
+
+        def load_scale_rows(engine, name, src, width):
+            dst = tile(name, [P, width], U8)
+            rows = src[0].bitcast(I32)
+            for q in range(4):
+                engine.dma_start(
+                    dst[32 * q : 32 * q + 32, :].bitcast(I32),
+                    rows[4 * q : 4 * q + 4, :].unsqueeze(0).to_broadcast([8, 4, width // 4]),
+                )
+            return dst
+
+        def load_words(name, src):
+            dst = tile(name, [P, TABLE], U32)
+            nc.sync.dma_start(dst[:].bitcast(I32), src[0].rearrange("p n r -> p (n r)").bitcast(I32))
+            return dst
+
+        def load_fp4(engine, name, src):
+            dst = tile(name, [P, 2 * S], U8)
+            engine.dma_start(dst[:].bitcast(I32), src[0].bitcast(I32))
+            return dst
+
+        def gather(name, window, offsets, dtype):
+            dst = tile(name, [P, S], dtype)
+            nc.vector.tensor_copy(dst[:], window[:].indirect(offsets[:]))
+            return dst
+
+        def deal(name, src, dtype, parts):
+            dst = tile(name, [P, S * parts], dtype)
+            nc.vector.tensor_copy(
+                dst[:].rearrange("p (t m b) -> p m t b", t=PACK, b=parts),
+                src[:].rearrange("p (m t b) -> p m t b", t=PACK, b=parts),
+            )
+            return dst
+
+        k1_t = load_list("k1_t", k1)
+        ds_table = tile("ds_table", [P, TABLE], U8)
+        nc.sync.dma_start(
+            ds_table[:].bitcast(I32),
+            d_scales[0].bitcast(I32).unsqueeze(1).to_broadcast([16, 8, TABLE // 4]),
+        )
+        offs_t = load_list("offs_t", offs)
+        xs_table = load_scale_rows(nc.sync, "xs_table", x_scales, TABLE)
+        xw_table = load_words("xw_table", x_words)
+        two_t = load_list("two_t", two)
+        w1w_raw = load_fp4(nc.sync, "w1w_raw", w1_words)
+        w1s_raw = load_scale_rows(nc.sync, "w1s_raw", w1_scales, S)
+        dw_table = load_words("dw_table", d_words)
+        n1_t = load_list("n1_t", n1)
+        n2_t = load_list("n2_t", n2)
+        gain = tile("gain", [P, PACK], F32)
+        nc.sync.dma_start(gain[:], gn.rearrange("(p t) o -> p (t o)", t=PACK))
+        n3_t = load_list("n3_t", n3)
+        n4_t = load_list("n4_t", n4)
+        w2w_raw = load_fp4(nc.sync, "w2w_raw", w2_words)
+        w2s_raw = load_scale_rows(nc.sync, "w2s_raw", w2_scales, S)
+
+        ds_picked = gather("ds_picked", ds_table, k1_t, U8)
+        ds_dealt = deal("ds_dealt", ds_picked, U8, 1)
+        for r in range(1, 4):
+            nc.scalar.dma_start(ds_dealt[r:P:32, :].bitcast(I32), ds_dealt[8 * r : P : 32, :].bitcast(I32))
+        xs_offs = gather("xs_offs", xs_table, offs_t, U8)
+        xs_two = gather("xs_two", xs_table, two_t, U8)
+        w1w = deal("w1w", w1w_raw, U8, 2)
+        w1s = deal("w1s", w1s_raw, U8, 1)
+        xw_offs = gather("xw_offs", xw_table, offs_t, U32)
+        dw_picked = gather("dw_picked", dw_table, k1_t, U32)
+        dw_dealt = deal("dw_dealt", dw_picked, U32, 1)
+        xw_two = tile("xw_two", [P, S], U32)
+        for u, cols in enumerate(halves):
+            nc.vector.tensor_copy(xw_two[:, cols], xw_table[:].indirect(two_t[:, 16 * u : 16 * u + 16]))
+
+        def product(lhs_words, lhs_dtype, parts, lhs_scales, t, rhs_words, rhs_scales, cols):
+            acc = bank(cols.stop - cols.start)
+            nc.tensor.matmul_mx(
+                acc[:],
+                lhsT=lhs_words[:, parts * P * t : parts * P * (t + 1)].bitcast(lhs_dtype),
+                lhsT_scale=lhs_scales[:, P * t : P * (t + 1)],
+                rhs=rhs_words[:, cols].bitcast(FP8X4),
+                rhs_scale=rhs_scales[:, cols],
+                start=True,
+                stop=True,
+            )
+            return acc
+
+        whole = slice(0, S)
+        order = (2, 0, 1, 3)
+        y_banks = {t: product(w1w, FP4X4, 2, w1s, t, xw_offs, xs_offs, whole) for t in order}
+        d_first = [product(dw_dealt, FP8X4, 1, ds_dealt, order[0], xw_two, xs_two, cols) for cols in halves]
+
+        def pair_tiles(name):
+            return [tile("%s_pairs%d" % (name, u), [P, 2, HALF, 2], BF16) for u in range(2)]
+
+        def round_rows(pairs, t, rows, factor):
+            for u, cols in enumerate(halves):
+                dst = pairs[u][:, t // 2, :, t % 2]
+                if t == order[-1]:
+                    nc.vector.tensor_scalar(dst, rows[:, cols], factor, None, MULT)
+                else:
+                    nc.scalar.activation(dst, rows[:, cols], COPY, scale=factor)
+
+        def quantise(name, pairs):
+            codes = tile(name + "_codes", [P, S], U32)
+            scales = tile(name + "_scales", [P, S], U8)
+            fours = [tile("%s_fours%d" % (name, u), [P, HALF, PACK], BF16) for u in range(2)]
+            for u in range(2):
+                nc.vector.tensor_copy(
+                    fours[u][:].bitcast(I32),
+                    pairs[u][:].rearrange("p v c e -> p v (c e)").bitcast(I32).rearrange("p v c -> p c v"),
+                )
+            for u, cols in enumerate(halves):
+                nc.vector.quantize_mx(
+                    codes[:, cols].bitcast(FP8X4), scales[:, cols], fours[u][:].rearrange("p c r -> p (c r)")
+                )
+            return codes, scales
+
+        z_pairs = pair_tiles("z")
+        ds_rows = {}
+        for t in order:
+            if t == order[-1]:
+                round_rows(z_pairs, order[0], ds_rows[order[0]], gain[:, order[0] : order[0] + 1])
+            y = tile("y%d" % t, [P, S], F32)
+            nc.scalar.activation(y[:], y_banks[t][:], COPY)
+            y_picked = tile("y_picked%d" % t, [P, W], F32)
+            nc.scalar.activation(y_picked[:], y[:].indirect(n1_t[:]), COPY, scale=-0.5)
+            d = tile("d%d" % t, [P, S], F32)
+            d_picked = tile("d_picked%d" % t, [P, W], F32)
+            if t == order[0]:
+                for u, cols in enumerate(halves):
+                    nc.vector.tensor_scalar(d[:, cols], d_first[u][:], 0.0625, None, MULT)
+                nc.vector.tensor_copy(d_picked[:], d[:].indirect(n2_t[:]))
+            else:
+                acc = product(dw_dealt, FP8X4, 1, ds_dealt, t, xw_two, xs_two, whole)
+                nc.scalar.activation(d[:], acc[:], COPY, scale=0.0625)
+                nc.scalar.activation(d_picked[:], d[:].indirect(n2_t[:]), COPY)
+            nc.vector.tensor_tensor(y[:].indirect(n1_t[:]), d_picked[:], y_picked[:], ADD)
+            ds_rows[t] = y
+        for t in order[1:]:
+            round_rows(z_pairs, t, ds_rows[t], gain[:, t : t + 1])
+
+        w2w = deal("w2w", w2w_raw, U8, 2)
+        w2s = deal("w2s", w2s_raw, U8, 1)
+        z_codes, z_scales = quantise("z", z_pairs)
+
+        out_rows = out_0.rearrange("(p t) j -> p t j", t=PACK)
+        out_pairs = pair_tiles("out")
+        h_rows = {}
+        for t in order:
+            if t == order[-1]:
+                round_rows(out_pairs, order[0], h_rows[order[0]], 1.0)
+            h = tile("h%d" % t, [P, S], F32)
+            pa = tile("pa%d" % t, [P, W], F32)
+            pb = tile("pb%d" % t, [P, W], F32)
+            if t == order[0]:
+                accs = [product(w2w, FP4X4, 2, w2s, t, z_codes, z_scales, cols) for cols in halves]
+                nc.scalar.copy(h[:, halves[0]], accs[0][:])
+                nc.vector.tensor_copy(h[:, halves[1]], accs[1][:])
+                nc.vector.tensor_copy(pa[:], h[:].indirect(n3_t[:]))
+            else:
+                acc = product(w2w, FP4X4, 2, w2s, t, z_codes, z_scales, whole)
+                nc.scalar.copy(h[:], acc[:])
+                nc.scalar.activation(pa[:], h[:].indirect(n3_t[:]), COPY)
+            nc.scalar.activation(pb[:], h[:].indirect(n4_t[:]), COPY)
+            larger = tile("larger%d" % t, [P, W], F32)
+            nc.vector.tensor_tensor(larger[:], pa[:], pb[:], MAX)
+            nc.vector.tensor_copy(h[:].indirect(n3_t[:]), larger[:])
+            nc.sync.dma_start(out_rows[:, t, :], h[:])
+            h_rows[t] = h
+        for t in order[1:]:
+            round_rows(out_pairs, t, h_rows[t], 1.0)
+
+        out_codes, out_scales = quantise("out", out_pairs)
+        words_out = out_1[0].rearrange("p n r -> p (n r)").bitcast(I32)
+        for cols in halves:
+            nc.sync.dma_start(words_out[:, cols], out_codes[:, cols].bitcast(I32))
+        scales_out = out_2[0].bitcast(I32)
+        for q in range(4):
+            engine = nc.sync if q % 2 == 0 else nc.scalar
+            engine.dma_start(scales_out[4 * q : 4 * q + 4, :], out_scales[32 * q : 32 * q + 4, :].bitcast(I32))

@@ -33,13 +33,13 @@ def tile_picked_twkeyputbfill_none_po_kernel(
 
     with ExitStack() as ctx:
         keep = ctx.enter_context(tc.tile_pool(name="keep", bufs=1))
-        psum = ctx.enter_context(tc.psum_pool(name="psum", bufs=8))
+        psum = ctx.enter_context(tc.psum_pool(name="psum", bufs=1))
 
-        def tile(name, shape, dtype):
-            return keep.tile(shape, dtype, name=name, align_bytes=64)
+        def tile(name, shape, dtype, tag=""):
+            return keep.tile(shape, dtype, name=name, tag=tag or name, align_bytes=64)
 
-        def bank(width):
-            return psum.tile([P, width], F32, name="bank")
+        def bank(number, width):
+            return psum.tile([P, width], F32, name="bank%d" % number)
 
         def load_list(name, src):
             dst = tile(name, list(src.shape), U16)
@@ -62,7 +62,7 @@ def tile_picked_twkeyputbfill_none_po_kernel(
             return dst
 
         def load_fp4(engine, name, src):
-            dst = tile(name, [P, 2 * S], U8)
+            dst = tile(name, [P, S], U16)
             engine.dma_start(dst[:].bitcast(I32), src[0].bitcast(I32))
             return dst
 
@@ -71,11 +71,19 @@ def tile_picked_twkeyputbfill_none_po_kernel(
             nc.vector.tensor_copy(dst[:], window[:].indirect(offsets[:]))
             return dst
 
-        def deal(name, src, dtype, parts):
-            dst = tile(name, [P, S * parts], dtype)
+        def deal_on_gpsimd(name, src, dtype, run, size):
+            dst = tile(name, [P, S], dtype)
+            nc.gpsimd.tensor_copy(
+                dst[:].bitcast(U8).rearrange("p (t c i b) -> p c t i b", t=PACK, i=run, b=size),
+                src[:].bitcast(U8).rearrange("p (c i t b) -> p c t i b", t=PACK, i=run, b=size),
+            )
+            return dst
+
+        def deal(name, src, dtype, run):
+            dst = tile(name, [P, S], dtype)
             nc.vector.tensor_copy(
-                dst[:].rearrange("p (t m b) -> p m t b", t=PACK, b=parts),
-                src[:].rearrange("p (m t b) -> p m t b", t=PACK, b=parts),
+                dst[:].rearrange("p (t c i) -> p c t i", t=PACK, i=run),
+                src[:].rearrange("p (c i t) -> p c t i", t=PACK, i=run),
             )
             return dst
 
@@ -88,9 +96,9 @@ def tile_picked_twkeyputbfill_none_po_kernel(
         offs_t = load_list("offs_t", offs)
         xs_table = load_scale_rows(nc.sync, "xs_table", x_scales, TABLE)
         xw_table = load_words("xw_table", x_words)
-        two_t = load_list("two_t", two)
         w1w_raw = load_fp4(nc.sync, "w1w_raw", w1_words)
         w1s_raw = load_scale_rows(nc.sync, "w1s_raw", w1_scales, S)
+        two_t = load_list("two_t", two)
         dw_table = load_words("dw_table", d_words)
         n1_t = load_list("n1_t", n1)
         n2_t = load_list("n2_t", n2)
@@ -102,25 +110,28 @@ def tile_picked_twkeyputbfill_none_po_kernel(
         w2s_raw = load_scale_rows(nc.sync, "w2s_raw", w2_scales, S)
 
         ds_picked = gather("ds_picked", ds_table, k1_t, U8)
-        ds_dealt = deal("ds_dealt", ds_picked, U8, 1)
+        ds_dealt = deal("ds_dealt", ds_picked, U8, 16)
         for r in range(1, 4):
-            nc.scalar.dma_start(ds_dealt[r:P:32, :].bitcast(I32), ds_dealt[8 * r : P : 32, :].bitcast(I32))
+            nc.sync.dma_start(ds_dealt[r:P:32, :].bitcast(I32), ds_dealt[8 * r : P : 32, :].bitcast(I32))
         xs_offs = gather("xs_offs", xs_table, offs_t, U8)
-        xs_two = gather("xs_two", xs_table, two_t, U8)
-        w1w = deal("w1w", w1w_raw, U8, 2)
-        w1s = deal("w1s", w1s_raw, U8, 1)
         xw_offs = gather("xw_offs", xw_table, offs_t, U32)
+        w1w = deal_on_gpsimd("w1w", w1w_raw, U16, 8, 2)
+        w1s = deal_on_gpsimd("w1s", w1s_raw, U8, 16, 1)
+        xs_two = gather("xs_two", xs_table, two_t, U8)
+        xw_two = gather("xw_two", xw_table, two_t, U32)
         dw_picked = gather("dw_picked", dw_table, k1_t, U32)
-        dw_dealt = deal("dw_dealt", dw_picked, U32, 1)
-        xw_two = tile("xw_two", [P, S], U32)
-        for u, cols in enumerate(halves):
-            nc.vector.tensor_copy(xw_two[:, cols], xw_table[:].indirect(two_t[:, 16 * u : 16 * u + 16]))
+        dw_dealt = tile("dw_dealt", [P, S], U32)
+        for ts in (slice(0, 1), slice(1, PACK)):
+            nc.vector.tensor_copy(
+                dw_dealt[:].rearrange("p (t c i) -> p c t i", t=PACK, i=4)[:, :, ts, :],
+                dw_picked[:].rearrange("p (c i t) -> p c t i", t=PACK, i=4)[:, :, ts, :],
+            )
 
-        def product(lhs_words, lhs_dtype, parts, lhs_scales, t, rhs_words, rhs_scales, cols):
-            acc = bank(cols.stop - cols.start)
+        def product(number, lhs_words, lhs_dtype, lhs_scales, t, rhs_words, rhs_scales, cols):
+            acc = bank(number, cols.stop - cols.start)
             nc.tensor.matmul_mx(
                 acc[:],
-                lhsT=lhs_words[:, parts * P * t : parts * P * (t + 1)].bitcast(lhs_dtype),
+                lhsT=lhs_words[:, P * t : P * (t + 1)].bitcast(lhs_dtype),
                 lhsT_scale=lhs_scales[:, P * t : P * (t + 1)],
                 rhs=rhs_words[:, cols].bitcast(FP8X4),
                 rhs_scale=rhs_scales[:, cols],
@@ -130,17 +141,19 @@ def tile_picked_twkeyputbfill_none_po_kernel(
             return acc
 
         whole = slice(0, S)
-        order = (2, 0, 1, 3)
-        y_banks = {t: product(w1w, FP4X4, 2, w1s, t, xw_offs, xs_offs, whole) for t in order}
-        d_first = [product(dw_dealt, FP8X4, 1, ds_dealt, order[0], xw_two, xs_two, cols) for cols in halves]
+        last = PACK - 1
+        y_banks = [product(t, w1w, FP4X4, w1s, t, xw_offs, xs_offs, whole) for t in range(last)]
+        d_first = [
+            product(3 + u, dw_dealt, FP8X4, ds_dealt, 0, xw_two, xs_two, cols) for u, cols in enumerate(halves)
+        ]
 
-        def pair_tiles(name):
-            return [tile("%s_pairs%d" % (name, u), [P, 2, HALF, 2], BF16) for u in range(2)]
+        def pair_tiles(name, tags):
+            return [tile("%s_pairs%d" % (name, u), [P, 2, HALF, 2], BF16, tags[u]) for u in range(2)]
 
-        def round_rows(pairs, t, rows, factor):
+        def round_rows(on_vector, pairs, t, rows, factor):
             for u, cols in enumerate(halves):
                 dst = pairs[u][:, t // 2, :, t % 2]
-                if t == order[-1]:
+                if on_vector:
                     nc.vector.tensor_scalar(dst, rows[:, cols], factor, None, MULT)
                 else:
                     nc.scalar.activation(dst, rows[:, cols], COPY, scale=factor)
@@ -151,8 +164,8 @@ def tile_picked_twkeyputbfill_none_po_kernel(
             fours = [tile("%s_fours%d" % (name, u), [P, HALF, PACK], BF16) for u in range(2)]
             for u in range(2):
                 nc.vector.tensor_copy(
-                    fours[u][:].bitcast(I32),
-                    pairs[u][:].rearrange("p v c e -> p v (c e)").bitcast(I32).rearrange("p v c -> p c v"),
+                    fours[u][:].bitcast(U32),
+                    pairs[u][:].rearrange("p v c e -> p v (c e)").bitcast(U32).rearrange("p v c -> p c v"),
                 )
             for u, cols in enumerate(halves):
                 nc.vector.quantize_mx(
@@ -160,60 +173,75 @@ def tile_picked_twkeyputbfill_none_po_kernel(
                 )
             return codes, scales
 
-        z_pairs = pair_tiles("z")
-        ds_rows = {}
-        for t in order:
-            if t == order[-1]:
-                round_rows(z_pairs, order[0], ds_rows[order[0]], gain[:, order[0] : order[0] + 1])
+        def y_rows(t, acc):
             y = tile("y%d" % t, [P, S], F32)
-            nc.scalar.activation(y[:], y_banks[t][:], COPY)
+            nc.scalar.activation(y[:], acc[:], COPY)
             y_picked = tile("y_picked%d" % t, [P, W], F32)
             nc.scalar.activation(y_picked[:], y[:].indirect(n1_t[:]), COPY, scale=-0.5)
+            return y, y_picked
+
+        ys = [y_rows(t, y_banks[t]) for t in range(last)]
+        for t in range(PACK):
+            if t == last:
+                ys.append(y_rows(t, product(3, w1w, FP4X4, w1s, t, xw_offs, xs_offs, whole)))
+            y, y_picked = ys[t]
             d = tile("d%d" % t, [P, S], F32)
             d_picked = tile("d_picked%d" % t, [P, W], F32)
-            if t == order[0]:
+            if t == 0:
                 for u, cols in enumerate(halves):
-                    nc.vector.tensor_scalar(d[:, cols], d_first[u][:], 0.0625, None, MULT)
-                nc.vector.tensor_copy(d_picked[:], d[:].indirect(n2_t[:]))
+                    nc.scalar.activation(d[:, cols], d_first[u][:], COPY, scale=0.0625)
+                nc.vector.tensor_copy(d_picked[:, 0:128], d[:].indirect(n2_t[:, 0:8]))
+                nc.scalar.activation(d_picked[:, 128:W], d[:].indirect(n2_t[:, 8:16]), COPY)
             else:
-                acc = product(dw_dealt, FP8X4, 1, ds_dealt, t, xw_two, xs_two, whole)
+                acc = product(4 + t, dw_dealt, FP8X4, ds_dealt, t, xw_two, xs_two, whole)
                 nc.scalar.activation(d[:], acc[:], COPY, scale=0.0625)
                 nc.scalar.activation(d_picked[:], d[:].indirect(n2_t[:]), COPY)
             nc.vector.tensor_tensor(y[:].indirect(n1_t[:]), d_picked[:], y_picked[:], ADD)
-            ds_rows[t] = y
-        for t in order[1:]:
-            round_rows(z_pairs, t, ds_rows[t], gain[:, t : t + 1])
+        z_pairs = pair_tiles("z", ("d3", "d2"))
+        for t in range(2, PACK):
+            round_rows(True, z_pairs, t, ys[t][0], gain[:, t : t + 1])
+        for t in range(2):
+            round_rows(False, z_pairs, t, ys[t][0], gain[:, t : t + 1])
 
-        w2w = deal("w2w", w2w_raw, U8, 2)
-        w2s = deal("w2s", w2s_raw, U8, 1)
+        w2w = deal("w2w", w2w_raw, U16, 8)
+        w2s = deal("w2s", w2s_raw, U8, 16)
         z_codes, z_scales = quantise("z", z_pairs)
 
         out_rows = out_0.rearrange("(p t) j -> p t j", t=PACK)
-        out_pairs = pair_tiles("out")
-        h_rows = {}
-        for t in order:
-            if t == order[-1]:
-                round_rows(out_pairs, order[0], h_rows[order[0]], 1.0)
+        h_rows = []
+        for t in range(PACK):
             h = tile("h%d" % t, [P, S], F32)
             pa = tile("pa%d" % t, [P, W], F32)
             pb = tile("pb%d" % t, [P, W], F32)
-            if t == order[0]:
-                accs = [product(w2w, FP4X4, 2, w2s, t, z_codes, z_scales, cols) for cols in halves]
+            larger = tile("larger%d" % t, [P, W], F32)
+            if t == 0:
+                accs = [
+                    product(u, w2w, FP4X4, w2s, t, z_codes, z_scales, cols) for u, cols in enumerate(halves)
+                ]
                 nc.scalar.copy(h[:, halves[0]], accs[0][:])
                 nc.vector.tensor_copy(h[:, halves[1]], accs[1][:])
-                nc.vector.tensor_copy(pa[:], h[:].indirect(n3_t[:]))
+                pieces = [(slice(128 * u, 128 * u + 128), slice(8 * u, 8 * u + 8)) for u in range(2)]
+                for part, cut in pieces:
+                    nc.vector.tensor_copy(pa[:, part], h[:].indirect(n3_t[:, cut]))
+                    nc.scalar.activation(pb[:, part], h[:].indirect(n4_t[:, cut]), COPY)
+                for part, cut in pieces:
+                    nc.vector.tensor_tensor(larger[:, part], pa[:, part], pb[:, part], MAX)
+                for part, cut in pieces:
+                    nc.vector.tensor_copy(h[:].indirect(n3_t[:, cut]), larger[:, part])
             else:
-                acc = product(w2w, FP4X4, 2, w2s, t, z_codes, z_scales, whole)
+                acc = product(1 + t, w2w, FP4X4, w2s, t, z_codes, z_scales, whole)
                 nc.scalar.copy(h[:], acc[:])
                 nc.scalar.activation(pa[:], h[:].indirect(n3_t[:]), COPY)
-            nc.scalar.activation(pb[:], h[:].indirect(n4_t[:]), COPY)
-            larger = tile("larger%d" % t, [P, W], F32)
-            nc.vector.tensor_tensor(larger[:], pa[:], pb[:], MAX)
-            nc.vector.tensor_copy(h[:].indirect(n3_t[:]), larger[:])
+                nc.scalar.activation(pb[:], h[:].indirect(n4_t[:]), COPY)
+                nc.vector.tensor_tensor(larger[:], pa[:], pb[:], MAX)
+                nc.vector.tensor_copy(h[:].indirect(n3_t[:]), larger[:])
             nc.sync.dma_start(out_rows[:, t, :], h[:])
-            h_rows[t] = h
-        for t in order[1:]:
-            round_rows(out_pairs, t, h_rows[t], 1.0)
+            h_rows.append(h)
+        out_pairs = pair_tiles("out", ("pa3", "pb3"))
+        for t in range(2, PACK):
+            round_rows(True, out_pairs, t, h_rows[t], 1.0)
+        for t in range(2):
+            round_rows(False, out_pairs, t, h_rows[t], 1.0)
 
         out_codes, out_scales = quantise("out", out_pairs)
         words_out = out_1[0].rearrange("p n r -> p (n r)").bitcast(I32)

from contextlib import ExitStack

import concourse.mybir as mybir

F32 = mybir.dt.float32
BF16 = mybir.dt.bfloat16
I32 = mybir.dt.int32
U32 = mybir.dt.uint32
U16 = mybir.dt.uint16
U8 = mybir.dt.uint8
FP8X4 = mybir.dt.float8_e4m3fn_x4
FP4X4 = mybir.dt.float4_e2m1fn_x4
COPY = mybir.ActivationFunctionType.Copy
ADD = mybir.AluOpType.add
MULT = mybir.AluOpType.mult
MAX = mybir.AluOpType.max

P = 128
PACK = 4
TABLE = 2048
S = 512
HALF = S // 2
W = 256
FLOPS = 3 * 2 * 512 * 512 * 512


def tile_picked_twkeyputbfill_none_po_kernel(
    tc, x_words, x_scales, w1_words, w1_scales, d_words, d_scales, gn, w2_words, w2_scales,
    offs, k1, two, n1, n2, n3, n4, out_0, out_1, out_2,
):
    nc = tc.nc
    halves = [slice(0, HALF), slice(HALF, S)]

    with ExitStack() as ctx:
        keep = ctx.enter_context(tc.tile_pool(name="keep", bufs=1))
        psum = ctx.enter_context(tc.psum_pool(name="psum", bufs=1))

        def tile(name, shape, dtype, tag=""):
            return keep.tile(shape, dtype, name=name, tag=tag or name, align_bytes=64)

        def bank(number, width):
            return psum.tile([P, width], F32, name="bank%d" % number)

        def load_list(name, src):
            dst = tile(name, list(src.shape), U16)
            nc.sync.dma_start(dst[:], src)
            return dst

        def load_scale_rows(engine, name, src, width):
            dst = tile(name, [P, width], U8)
            rows = src[0].bitcast(I32)
            for q in range(4):
                engine.dma_start(
                    dst[32 * q : 32 * q + 32, :].bitcast(I32),
                    rows[4 * q : 4 * q + 4, :].unsqueeze(0).to_broadcast([8, 4, width // 4]),
                )
            return dst

        def load_words(name, src):
            dst = tile(name, [P, TABLE], U32)
            nc.sync.dma_start(dst[:].bitcast(I32), src[0].rearrange("p n r -> p (n r)").bitcast(I32))
            return dst

        def load_fp4(engine, name, src):
            dst = tile(name, [P, S], U16)
            engine.dma_start(dst[:].bitcast(I32), src[0].bitcast(I32))
            return dst

        def gather(name, window, offsets, dtype):
            dst = tile(name, [P, S], dtype)
            nc.vector.tensor_copy(dst[:], window[:].indirect(offsets[:]))
            return dst

        def deal_on_gpsimd(name, src, dtype, run, size):
            dst = tile(name, [P, S], dtype)
            nc.gpsimd.tensor_copy(
                dst[:].bitcast(U8).rearrange("p (t c i b) -> p c t i b", t=PACK, i=run, b=size),
                src[:].bitcast(U8).rearrange("p (c i t b) -> p c t i b", t=PACK, i=run, b=size),
            )
            return dst

        def deal(name, src, dtype, run):
            dst = tile(name, [P, S], dtype)
            nc.vector.tensor_copy(
                dst[:].rearrange("p (t c i) -> p c t i", t=PACK, i=run),
                src[:].rearrange("p (c i t) -> p c t i", t=PACK, i=run),
            )
            return dst

        k1_t = load_list("k1_t", k1)
        ds_table = tile("ds_table", [P, TABLE], U8)
        nc.sync.dma_start(
            ds_table[:].bitcast(I32),
            d_scales[0].bitcast(I32).unsqueeze(1).to_broadcast([16, 8, TABLE // 4]),
        )
        offs_t = load_list("offs_t", offs)
        xs_table = load_scale_rows(nc.sync, "xs_table", x_scales, TABLE)
        xw_table = load_words("xw_table", x_words)
        w1w_raw = load_fp4(nc.sync, "w1w_raw", w1_words)
        w1s_raw = load_scale_rows(nc.sync, "w1s_raw", w1_scales, S)
        two_t = load_list("two_t", two)
        dw_table = load_words("dw_table", d_words)
        n1_t = load_list("n1_t", n1)
        n2_t = load_list("n2_t", n2)
        gain = tile("gain", [P, PACK], F32)
        nc.sync.dma_start(gain[:], gn.rearrange("(p t) o -> p (t o)", t=PACK))
        n3_t = load_list("n3_t", n3)
        n4_t = load_list("n4_t", n4)
        w2w_raw = load_fp4(nc.sync, "w2w_raw", w2_words)
        w2s_raw = load_scale_rows(nc.sync, "w2s_raw", w2_scales, S)

        ds_picked = gather("ds_picked", ds_table, k1_t, U8)
        ds_dealt = deal("ds_dealt", ds_picked, U8, 16)
        for r in range(1, 4):
            nc.sync.dma_start(ds_dealt[r:P:32, :].bitcast(I32), ds_dealt[8 * r : P : 32, :].bitcast(I32))
        xs_offs = gather("xs_offs", xs_table, offs_t, U8)
        xw_offs = gather("xw_offs", xw_table, offs_t, U32)
        w1w = deal_on_gpsimd("w1w", w1w_raw, U16, 8, 2)
        w1s = deal_on_gpsimd("w1s", w1s_raw, U8, 16, 1)
        xs_two = gather("xs_two", xs_table, two_t, U8)
        xw_two = gather("xw_two", xw_table, two_t, U32)
        dw_picked = gather("dw_picked", dw_table, k1_t, U32)
        dw_dealt = tile("dw_dealt", [P, S], U32)
        for ts in (slice(0, 1), slice(1, PACK)):
            nc.vector.tensor_copy(
                dw_dealt[:].rearrange("p (t c i) -> p c t i", t=PACK, i=4)[:, :, ts, :],
                dw_picked[:].rearrange("p (c i t) -> p c t i", t=PACK, i=4)[:, :, ts, :],
            )

        def product(number, lhs_words, lhs_dtype, lhs_scales, t, rhs_words, rhs_scales, cols):
            acc = bank(number, cols.stop - cols.start)
            nc.tensor.matmul_mx(
                acc[:],
                lhsT=lhs_words[:, P * t : P * (t + 1)].bitcast(lhs_dtype),
                lhsT_scale=lhs_scales[:, P * t : P * (t + 1)],
                rhs=rhs_words[:, cols].bitcast(FP8X4),
                rhs_scale=rhs_scales[:, cols],
                start=True,
                stop=True,
            )
            return acc

        whole = slice(0, S)
        last = PACK - 1
        y_banks = [product(t, w1w, FP4X4, w1s, t, xw_offs, xs_offs, whole) for t in range(last)]
        d_first = [
            product(3 + u, dw_dealt, FP8X4, ds_dealt, 0, xw_two, xs_two, cols) for u, cols in enumerate(halves)
        ]

        def pair_tiles(name, tags):
            return [tile("%s_pairs%d" % (name, u), [P, 2, HALF, 2], BF16, tags[u]) for u in range(2)]

        def round_rows(on_vector, pairs, t, rows, factor):
            for u, cols in enumerate(halves):
                dst = pairs[u][:, t // 2, :, t % 2]
                if on_vector:
                    nc.vector.tensor_scalar(dst, rows[:, cols], factor, None, MULT)
                else:
                    nc.scalar.activation(dst, rows[:, cols], COPY, scale=factor)

        def quantise(name, pairs):
            codes = tile(name + "_codes", [P, S], U32)
            scales = tile(name + "_scales", [P, S], U8)
            fours = [tile("%s_fours%d" % (name, u), [P, HALF, PACK], BF16) for u in range(2)]
            for u in range(2):
                nc.vector.tensor_copy(
                    fours[u][:].bitcast(U32),
                    pairs[u][:].rearrange("p v c e -> p v (c e)").bitcast(U32).rearrange("p v c -> p c v"),
                )
            for u, cols in enumerate(halves):
                nc.vector.quantize_mx(
                    codes[:, cols].bitcast(FP8X4), scales[:, cols], fours[u][:].rearrange("p c r -> p (c r)")
                )
            return codes, scales

        def y_rows(t, acc):
            y = tile("y%d" % t, [P, S], F32)
            nc.scalar.activation(y[:], acc[:], COPY)
            y_picked = tile("y_picked%d" % t, [P, W], F32)
            nc.scalar.activation(y_picked[:], y[:].indirect(n1_t[:]), COPY, scale=-0.5)
            return y, y_picked

        ys = [y_rows(t, y_banks[t]) for t in range(last)]
        for t in range(PACK):
            if t == last:
                ys.append(y_rows(t, product(3, w1w, FP4X4, w1s, t, xw_offs, xs_offs, whole)))
            y, y_picked = ys[t]
            d = tile("d%d" % t, [P, S], F32)
            d_picked = tile("d_picked%d" % t, [P, W], F32)
            if t == 0:
                for u, cols in enumerate(halves):
                    nc.scalar.activation(d[:, cols], d_first[u][:], COPY, scale=0.0625)
                nc.vector.tensor_copy(d_picked[:, 0:128], d[:].indirect(n2_t[:, 0:8]))
                nc.scalar.activation(d_picked[:, 128:W], d[:].indirect(n2_t[:, 8:16]), COPY)
            else:
                acc = product(4 + t, dw_dealt, FP8X4, ds_dealt, t, xw_two, xs_two, whole)
                nc.scalar.activation(d[:], acc[:], COPY, scale=0.0625)
                nc.scalar.activation(d_picked[:], d[:].indirect(n2_t[:]), COPY)
            nc.vector.tensor_tensor(y[:].indirect(n1_t[:]), d_picked[:], y_picked[:], ADD)
        z_pairs = pair_tiles("z", ("d3", "d2"))
        for t in range(2, PACK):
            round_rows(True, z_pairs, t, ys[t][0], gain[:, t : t + 1])
        for t in range(2):
            round_rows(False, z_pairs, t, ys[t][0], gain[:, t : t + 1])

        w2w = deal("w2w", w2w_raw, U16, 8)
        w2s = deal("w2s", w2s_raw, U8, 16)
        z_codes, z_scales = quantise("z", z_pairs)

        out_rows = out_0.rearrange("(p t) j -> p t j", t=PACK)
        h_rows = []
        for t in range(PACK):
            h = tile("h%d" % t, [P, S], F32)
            pa = tile("pa%d" % t, [P, W], F32)
            pb = tile("pb%d" % t, [P, W], F32)
            larger = tile("larger%d" % t, [P, W], F32)
            if t == 0:
                accs = [
                    product(u, w2w, FP4X4, w2s, t, z_codes, z_scales, cols) for u, cols in enumerate(halves)
                ]
                nc.scalar.copy(h[:, halves[0]], accs[0][:])
                nc.vector.tensor_copy(h[:, halves[1]], accs[1][:])
                pieces = [(slice(128 * u, 128 * u + 128), slice(8 * u, 8 * u + 8)) for u in range(2)]
                for part, cut in pieces:
                    nc.vector.tensor_copy(pa[:, part], h[:].indirect(n3_t[:, cut]))
                    nc.scalar.activation(pb[:, part], h[:].indirect(n4_t[:, cut]), COPY)
                for part, cut in pieces:
                    nc.vector.tensor_tensor(larger[:, part], pa[:, part], pb[:, part], MAX)
                for part, cut in pieces:
                    nc.vector.tensor_copy(h[:].indirect(n3_t[:, cut]), larger[:, part])
            else:
                acc = product(1 + t, w2w, FP4X4, w2s, t, z_codes, z_scales, whole)
                nc.scalar.copy(h[:], acc[:])
                nc.scalar.activation(pa[:], h[:].indirect(n3_t[:]), COPY)
                nc.scalar.activation(pb[:], h[:].indirect(n4_t[:]), COPY)
                nc.vector.tensor_tensor(larger[:], pa[:], pb[:], MAX)
                nc.vector.tensor_copy(h[:].indirect(n3_t[:]), larger[:])
            nc.sync.dma_start(out_rows[:, t, :], h[:])
            h_rows.append(h)
        out_pairs = pair_tiles("out", ("pa3", "pb3"))
        for t in range(2, PACK):
            round_rows(True, out_pairs, t, h_rows[t], 1.0)
        for t in range(2):
            round_rows(False, out_pairs, t, h_rows[t], 1.0)

        out_codes, out_scales = quantise("out", out_pairs)
        words_out = out_1[0].rearrange("p n r -> p (n r)").bitcast(I32)
        for cols in halves:
            nc.sync.dma_start(words_out[:, cols], out_codes[:, cols].bitcast(I32))
        scales_out = out_2[0].bitcast(I32)
        for q in range(4):
            engine = nc.sync if q % 2 == 0 else nc.scalar
            engine.dma_start(scales_out[4 * q : 4 * q + 4, :], out_scales[32 * q : 32 * q + 4, :].bitcast(I32))
